import numpy as np
import ml_dtypes


def mxq(x, axis, fmt="e4m3"):
    dtype, down = {"e4m3": (ml_dtypes.float8_e4m3fn, 7), "e5m2": (ml_dtypes.float8_e5m2, 14)}[fmt]
    v = np.moveaxis(np.asarray(x, np.float32).astype(ml_dtypes.bfloat16).astype(np.float64), axis, -1)
    blocks = v.reshape(v.shape[:-1] + (-1, 32))
    amax = np.abs(blocks).max(-1, keepdims=True)
    byte = np.maximum(np.where(amax > 0, np.frexp(amax)[1] - 1 + 127, 0) - down, 1)
    scale = np.exp2(byte - 127.0)
    codes = (blocks / scale).astype(np.float32).astype(dtype).astype(np.float64)
    return np.moveaxis((codes * scale).reshape(v.shape), -1, axis)


WIDE = False


def mx_kscale(k):
    if not WIDE:
        return np.ones(k)
    levels = np.array([24, -24, 12, -12, 0])
    if k % 512:
        return np.exp2(np.random.permutation(np.resize(levels, k // 32))).repeat(32)
    a = np.empty((k // 512, 16))
    for p in range(k // 512):
        a[p, :8] = np.random.permutation(np.resize(levels, 8))
        for g in range(8):
            far = levels[np.abs(levels - a[p, g]) >= 10]
            a[p, g + 8] = far[np.random.randint(len(far))]
    return np.exp2(a.ravel()).repeat(32)


def f64(x):
    return np.asarray(x).astype(np.float64)


def striped(idx):
    return np.tile(idx.reshape(-1, 16).T, (8, 1)).astype(np.uint16)


def unstriped(offs):
    return offs[:16].T.reshape(-1).astype(np.int64)


E2M1 = np.array([0.0, 0.5, 1.0, 1.5, 2.0, 3.0, 4.0, 6.0, -0.0, -0.5, -1.0, -1.5, -2.0, -3.0, -4.0, -6.0])


def pack_weight(w, fmt):
    k, n = w.shape
    w = f64(np.asarray(w, np.float32).astype(ml_dtypes.bfloat16)).reshape(k // 32, 32, n)
    amax = np.abs(w).max(1)
    if fmt == "e4m3":
        byte = np.frexp(amax)[1] - 1 + 127 - 7
    else:
        mant, ex = np.frexp(amax / 6.0)
        byte = np.where(mant > 0.5, ex, ex - 1) + 127
    byte = np.clip(np.where(amax > 0, byte, 1), 1, 254)
    scaled = (w * np.exp2(127.0 - byte)[:, None, :]).reshape(k, n).astype(np.float32)
    by_word = np.ascontiguousarray(scaled.reshape(k // 512, 128, 4, n).transpose(0, 1, 3, 2))
    if fmt == "e4m3":
        words = by_word.astype(ml_dtypes.float8_e4m3fn).view(np.uint8)
    else:
        c = by_word.astype(ml_dtypes.float4_e2m1fn).view(np.uint8) & 0xF
        words = (c[..., 0::2] | (c[..., 1::2] << 4)).reshape(k // 512, 128, 2 * n)
    return np.ascontiguousarray(words), np.ascontiguousarray(byte.astype(np.uint8).reshape(k // 512, 16, n))


def unpack_weight(words, scales, fmt):
    g, _, n = scales.shape
    words = np.ascontiguousarray(words).reshape(g, 128, n, -1)
    if fmt == "e4m3":
        vals = words.view(ml_dtypes.float8_e4m3fn).astype(np.float64)
    else:
        nib = np.empty((g, 128, n, 4), np.uint8)
        nib[..., 0::2] = words & 0xF
        nib[..., 1::2] = words >> 4
        vals = E2M1[nib]
    vals = vals * np.repeat(np.exp2(scales.astype(np.float64) - 127.0), 8, axis=1)[..., None]
    return vals.transpose(0, 1, 3, 2).reshape(g * 512, n)


def pack_table4(v):
    words, scales = pack_weight(v, "e2m1")
    g, t = words.shape[0] // 2, v.shape[1]
    return np.ascontiguousarray(words.reshape(g, 2, 128, t, 2).transpose(0, 2, 3, 1, 4).reshape(g, 128, t, 4)), scales


def unpack_table4(words, scales):
    g, _, t, _ = words.shape
    return unpack_weight(words.reshape(g, 128, t, 2, 2).transpose(0, 3, 1, 2, 4).reshape(2 * g, 128, 2 * t), scales, "e2m1")


def sigm(f):
    return 1.0 / (1.0 + np.exp(-np.maximum(f, -700.0)))


def gelu(f):
    return 0.5 * f * (1.0 + np.tanh(np.sqrt(2.0 / np.pi) * (f + 0.044715 * f**3)))


K, L, R, N, T, J = 512, 1024, 512, 512, 1024, 512


def setup_inputs():
    n = np.random.standard_normal
    s = mx_kscale(K)[:, None]
    s2 = mx_kscale(L)[:, None]
    u = mx_kscale(R)[:, None]
    p_tab = pack_weight(n((K, T)) * s, "e4m3")
    p_tab2 = pack_table4(n((L, T)) * s2)
    p_wa = pack_weight(n((K, R)) / np.sqrt(K) / s * u.T, "e2m1")
    p_wb = pack_weight(n((L, R)) / np.sqrt(L) / s2, "e2m1")
    return {
        "tab_words": p_tab[0],
        "tab_scales": p_tab[1],
        "tab2_words": p_tab2[0],
        "tab2_scales": p_tab2[1],
        "wa_words": p_wa[0],
        "wa_scales": p_wa[1],
        "wb_words": p_wb[0],
        "wb_scales": p_wb[1],
        "en": (n((R, N)) / np.sqrt(R) / u).astype(np.float32),
        "b": (0.3 * n(N)).astype(np.float32),
        "offs": striped(np.random.permutation(T)[:J]),
        "offs2": striped(np.random.permutation(T)[:J]),
    }


def reference(tab_words, tab_scales, tab2_words, tab2_scales, wa_words, wa_scales, wb_words, wb_scales, en, b, offs, offs2):
    idx = unstriped(offs)
    idx2 = unstriped(offs2)
    tab_ = unpack_weight(tab_words, tab_scales, "e4m3")[:, idx]
    tab2_ = unpack_table4(tab2_words, tab2_scales)[:, idx2]
    wa_ = unpack_weight(wa_words, wa_scales, "e2m1")
    wb_ = unpack_weight(wb_words, wb_scales, "e2m1")
    ha = wa_.T @ tab_
    hb = wb_.T @ tab2_
    h = ha * sigm(hb)
    h_ = mxq(h, 0, "e4m3")
    en_ = mxq(f64(en), 0, "e4m3")
    y = en_.T @ h_
    return gelu(y + f64(b)[:, None])

@@ -1,0 +1,199 @@
+from contextlib import ExitStack
+
+import concourse.mybir as mybir
+
+F32 = mybir.dt.float32
+BF16 = mybir.dt.bfloat16
+I32 = mybir.dt.int32
+U32 = mybir.dt.uint32
+U16 = mybir.dt.uint16
+U8 = mybir.dt.uint8
+FP8X4 = mybir.dt.float8_e4m3fn_x4
+FP4X4 = mybir.dt.float4_e2m1fn_x4
+ACT = mybir.ActivationFunctionType
+ALU = mybir.AluOpType
+
+K, L, R, N, T, J = 512, 1024, 512, 512, 1024, 512
+P = 128
+CH = 128
+NCH = J // CH
+FLOPS = 2 * J * (K * R + L * R + R * N)
+
+
+def tile_list_kg_gate_gelu_kernel(
+    tc, tab_words, tab_scales, tab2_words, tab2_scales, wa_words, wa_scales, wb_words, wb_scales, en, b, offs, offs2, out
+):
+    nc = tc.nc
+    with ExitStack() as ctx:
+        keep = ctx.enter_context(tc.tile_pool(name="keep", bufs=1))
+        psum = ctx.enter_context(tc.psum_pool(name="psum", bufs=1))
+
+        list1 = keep.tile([P, J // 16], U16, name="list1")
+        list2 = keep.tile([P, J // 16], U16, name="list2")
+        win2s = keep.tile([P, T], U8, name="win2s", align_bytes=64)
+        win1s = keep.tile([P, T], U8, name="win1s", align_bytes=64)
+        win2w = keep.tile([P, T], I32, name="win2w", align_bytes=64)
+        win1w = keep.tile([P, T], I32, name="win1w", align_bytes=64)
+        ws_raw = keep.tile([32, 2, R], U8, name="ws_raw", align_bytes=64)
+        wb_raw = keep.tile([P, 2, R // 2], I32, name="wb_raw", align_bytes=64)
+        wa_raw = keep.tile([P, R // 2], I32, name="wa_raw", align_bytes=64)
+        en_raw = keep.tile([P, 4, N], F32, name="en_raw", align_bytes=64)
+        bias = keep.tile([P, 4], F32, name="bias")
+        zin = keep.tile([P, 1], F32, name="zin")
+        zero = keep.tile([P, 1], F32, name="zero")
+        planes = keep.tile([P, 8, 512], U8, name="planes", align_bytes=64)
+        stage = keep.tile([32, 4, 512], U8, name="stage", align_bytes=64)
+        g2s = keep.tile([P, J], U8, name="g2s", align_bytes=64)
+        g1s = keep.tile([P, J], U8, name="g1s", align_bytes=64)
+        wb_p = keep.tile([P, 2, 4, 64], I32, name="wb_p", align_bytes=64)
+        wa_p = keep.tile([P, 4, 64], I32, name="wa_p", align_bytes=64)
+        en_bf = keep.tile([P, N, 4], BF16, name="en_bf", align_bytes=64)
+        en_q = keep.tile([P, N], U32, name="en_q", align_bytes=64)
+        en_s = keep.tile([P, N], U8, name="en_s", align_bytes=64)
+
+        for win in (win2s, win1s):
+            nc.vector.memset(win[32:64, :].bitcast(I32), 0)
+            nc.vector.memset(win[64:128, :].bitcast(I32), 0)
+        nc.vector.memset(zin[:], 0.0)
+        nc.vector.memset(planes[:, 0:6, :].rearrange("p a r -> p (a r)").bitcast(I32), 0)
+
+        nc.sync.dma_start(list2[:], offs2)
+        nc.sync.dma_start(out=win2s[0:32, :].bitcast(I32), in_=tab2_scales.rearrange("a q t -> q a t").bitcast(I32))
+        nc.sync.dma_start(list1[:], offs)
+        nc.sync.dma_start(
+            out=win1s[0:32, :].bitcast(I32), in_=tab_scales[0].bitcast(I32).unsqueeze(1).broadcast_to([16, 2, T // 4])
+        )
+        nc.sync.dma_start(out=ws_raw[:, 0, :].bitcast(I32), in_=wb_scales.rearrange("a q r -> q a r").bitcast(I32))
+        nc.sync.dma_start(
+            out=ws_raw[:, 1, :].bitcast(I32), in_=wa_scales[0].bitcast(I32).unsqueeze(1).broadcast_to([16, 2, R // 4])
+        )
+        nc.sync.dma_start(out=win2w[:], in_=tab2_words[0].rearrange("p t i -> p (t i)").bitcast(I32))
+        en_v = en.rearrange("(u t e) n -> e u t n", t=4, e=2)
+        for e in range(2):
+            nc.sync.dma_start(out=en_raw[e:P:2, :, :], in_=en_v[e])
+        nc.sync.dma_start(out=wb_raw[:], in_=wb_words.rearrange("a p c -> p a c").bitcast(I32))
+        nc.sync.dma_start(out=win1w[:], in_=tab_words[0].rearrange("p t i -> p (t i)").bitcast(I32))
+        nc.sync.dma_start(out=wa_raw[:], in_=wa_words[0].bitcast(I32))
+        nc.gpsimd.dma_start(out=bias[:], in_=b.rearrange("(p m) -> p m", m=4))
+
+        nc.scalar.activation(out=zero[:], in_=zin[:], func=ACT.Gelu_apprx_tanh)
+
+        nc.vector.tensor_copy(g2s[:], win2s[:].indirect(list2[:]))
+        nc.vector.tensor_copy(g1s[:], win1s[:].indirect(list1[:]))
+        nc.vector.tensor_copy(
+            out=stage[:, 1:4:2, :].bitcast(U16).rearrange("p a (t c i) -> p a c t i", t=4, i=4),
+            in_=ws_raw[:].bitcast(U16).rearrange("p a (c i t) -> p a c t i", t=4, i=4),
+        )
+        nc.vector.tensor_copy(out=stage[:, 0, :].bitcast(I32), in_=g2s[0:32, :].bitcast(I32))
+        nc.vector.tensor_copy(out=stage[:, 2, :].bitcast(I32), in_=g1s[0:32, :].bitcast(I32))
+        for q in range(4):
+            nc.scalar.dma_start(
+                out=planes[32 * q : 32 * q + 4, :, :].rearrange("p (a s) r -> p a (s r)", a=2).bitcast(I32),
+                in_=stage[8 * q : 8 * q + 8, :, :].rearrange("p s r -> p (s r)").bitcast(I32),
+            )
+
+        cols = CH // 16
+        g2w, p2w, g1w = [], [], []
+        for c in range(NCH):
+            g = keep.tile([P, CH], U32, name="g2w%d" % c, align_bytes=64)
+            nc.vector.tensor_copy(g[:], win2w[:].bitcast(U32).indirect(list2[:, c * cols : (c + 1) * cols]))
+            g2w.append(g)
+        nc.vector.tensor_copy(
+            out=wb_p[:].rearrange("p a t (c i) -> p a c t i", i=4),
+            in_=wb_raw[:].rearrange("p a (c i t) -> p a c t i", t=4, i=4),
+        )
+        for c in range(NCH):
+            pw = keep.tile([P, 2, CH], U16, name="p2w%d" % c, align_bytes=64)
+            nc.vector.tensor_copy(out=pw[:], in_=g2w[c][:].bitcast(U16).rearrange("p (j d) -> p d j", d=2))
+            p2w.append(pw)
+
+        for k in range(4):
+            nc.scalar.copy(
+                out=en_bf[:].rearrange("p (m c) t -> p c t m", m=4)[:, 32 * k : 32 * k + 32, :, :],
+                in_=en_raw[:].rearrange("p t (c m) -> p c t m", m=4)[:, 32 * k : 32 * k + 32, :, :],
+            )
+
+        th = []
+        for c in range(NCH):
+            js = slice(c * CH, (c + 1) * CH)
+            hb = psum.tile([P, 4, CH], F32, name="hb", tag="hb", bufs=3)
+            for t in range(4):
+                for a in range(2):
+                    nc.tensor.matmul_mx(
+                        out=hb[:, t, :],
+                        lhsT=wb_p[:, a, t, :].bitcast(FP4X4),
+                        lhsT_scale=planes[:, 4 * a + 1, t * P : (t + 1) * P],
+                        rhs=p2w[c][:, a, :].bitcast(FP4X4),
+                        rhs_scale=planes[:, 4 * a, js],
+                        start=(a == 0),
+                        stop=(a == 1),
+                    )
+            tt = keep.tile([P, CH, 4], F32, name="th%d" % c, align_bytes=64)
+            nc.scalar.activation(
+                out=tt[:], in_=hb[:].rearrange("p t j -> p j t"), func=ACT.Tanh, scale=0.5, bias=zero[:]
+            )
+            th.append(tt)
+
+        nc.vector.tensor_copy(
+            out=wa_p[:].rearrange("p t (c i) -> p c t i", i=4),
+            in_=wa_raw[:].rearrange("p (c i t) -> p c t i", t=4, i=4),
+        )
+        for c in range(NCH):
+            g = keep.tile([P, CH], U32, name="g1w%d" % c, align_bytes=64)
+            nc.vector.tensor_copy(g[:], win1w[:].bitcast(U32).indirect(list1[:, c * cols : (c + 1) * cols]))
+            g1w.append(g)
+        nc.vector.quantize_mx(out=en_q[:].bitcast(FP8X4), scales=en_s[:], in_=en_bf[:].rearrange("p n t -> p (n t)"))
+
+        ha = []
+        for c in range(NCH):
+            js = slice(c * CH, (c + 1) * CH)
+            acc = psum.tile([P, 4, CH], F32, name="ha", tag="ha", bufs=3)
+            for t in range(4):
+                nc.tensor.matmul_mx(
+                    out=acc[:, t, :],
+                    lhsT=wa_p[:, t, :].bitcast(FP4X4),
+                    lhsT_scale=planes[:, 3, t * P : (t + 1) * P],
+                    rhs=g1w[c][:].bitcast(FP8X4),
+                    rhs_scale=planes[:, 2, js],
+                    start=True,
+                    stop=True,
+                )
+            ha.append(acc)
+
+        out_v = out.rearrange("(p m) j -> p m j", m=4)
+        hbf = []
+
+        def gate(c):
+            h = keep.tile([P, CH, 4], BF16, name="h%d" % c, align_bytes=64)
+            nc.vector.scalar_tensor_tensor(
+                out=h[:], in0=th[c][:], scalar=1.0, in1=ha[c][:].rearrange("p t j -> p j t"), op0=ALU.add, op1=ALU.mult
+            )
+            hbf.append(h)
+
+        def score(c):
+            hq = keep.tile([P, CH], U32, name="hq%d" % c, align_bytes=64)
+            hs = keep.tile([P, CH], U8, name="hs%d" % c, align_bytes=64)
+            nc.vector.quantize_mx(out=hq[:].bitcast(FP8X4), scales=hs[:], in_=hbf[c][:].rearrange("p j t -> p (j t)"))
+            y = psum.tile([P, 4, CH], F32, name="y", tag="y", bufs=2)
+            res = keep.tile([P, 4, CH], F32, name="res%d" % c, align_bytes=64)
+            for m in range(4):
+                nc.tensor.matmul_mx(
+                    out=y[:, m, :],
+                    lhsT=en_q[:, m * P : (m + 1) * P].bitcast(FP8X4),
+                    lhsT_scale=en_s[:, m * P : (m + 1) * P],
+                    rhs=hq[:].bitcast(FP8X4),
+                    rhs_scale=hs[:],
+                    start=True,
+                    stop=True,
+                )
+            for m in range(4):
+                nc.scalar.activation(
+                    out=res[:, m, :], in_=y[:, m, :], func=ACT.Gelu_apprx_tanh, scale=0.5, bias=bias[:, m : m + 1]
+                )
+            nc.sync.dma_start(out=out_v[:, :, c * CH : (c + 1) * CH], in_=res[:])
+
+        gate(0)
+        for c in range(1, NCH):
+            gate(c)
+            score(c - 1)
+        score(NCH - 1)

@@ -34,15 +34,14 @@ def tile_list_kg_gate_gelu_kernel(
         win1s = keep.tile([P, T], U8, name="win1s", align_bytes=64)
         win2w = keep.tile([P, T], I32, name="win2w", align_bytes=64)
         win1w = keep.tile([P, T], I32, name="win1w", align_bytes=64)
-        ws_raw = keep.tile([32, 2, R], U8, name="ws_raw", align_bytes=64)
+        ws_raw = keep.tile([32, 2, R], U8, name="ws_raw", tag="ws_then_bias", align_bytes=64)
         wb_raw = keep.tile([P, 2, R // 2], I32, name="wb_raw", align_bytes=64)
         wa_raw = keep.tile([P, R // 2], I32, name="wa_raw", align_bytes=64)
         en_raw = keep.tile([P, 4, N], F32, name="en_raw", align_bytes=64)
-        bias = keep.tile([P, 4], F32, name="bias")
         zin = keep.tile([P, 1], F32, name="zin")
         zero = keep.tile([P, 1], F32, name="zero")
-        planes = keep.tile([P, 8, 512], U8, name="planes", align_bytes=64)
-        stage = keep.tile([32, 4, 512], U8, name="stage", align_bytes=64)
+        planes = keep.tile([P, 6, 512], U8, name="planes", align_bytes=64)
+        stage = keep.tile([32, 3, 512], U8, name="stage", align_bytes=64)
         g2s = keep.tile([P, J], U8, name="g2s", align_bytes=64)
         g1s = keep.tile([P, J], U8, name="g1s", align_bytes=64)
         wb_p = keep.tile([P, 2, 4, 64], I32, name="wb_p", align_bytes=64)
@@ -51,80 +50,78 @@ def tile_list_kg_gate_gelu_kernel(
         en_q = keep.tile([P, N], U32, name="en_q", align_bytes=64)
         en_s = keep.tile([P, N], U8, name="en_s", align_bytes=64)
 
-        for win in (win2s, win1s):
-            nc.vector.memset(win[32:64, :].bitcast(I32), 0)
-            nc.vector.memset(win[64:128, :].bitcast(I32), 0)
+        nc.vector.memset(win2s[32:64, :].bitcast(I32), 0)
+        nc.vector.memset(win2s[64:128, :].bitcast(I32), 0)
+        nc.gpsimd.memset(win1s[:].bitcast(I32), 0)
         nc.vector.memset(zin[:], 0.0)
-        nc.vector.memset(planes[:, 0:6, :].rearrange("p a r -> p (a r)").bitcast(I32), 0)
 
         nc.sync.dma_start(list2[:], offs2)
+        nc.scalar.dma_start(out=win2w[:], in_=tab2_words[0].rearrange("p t i -> p (t i)").bitcast(I32))
         nc.sync.dma_start(out=win2s[0:32, :].bitcast(I32), in_=tab2_scales.rearrange("a q t -> q a t").bitcast(I32))
-        nc.sync.dma_start(list1[:], offs)
-        nc.sync.dma_start(
-            out=win1s[0:32, :].bitcast(I32), in_=tab_scales[0].bitcast(I32).unsqueeze(1).broadcast_to([16, 2, T // 4])
-        )
+        nc.scalar.dma_start(out=wb_raw[:], in_=wb_words.rearrange("a p c -> p a c").bitcast(I32))
         nc.sync.dma_start(out=ws_raw[:, 0, :].bitcast(I32), in_=wb_scales.rearrange("a q r -> q a r").bitcast(I32))
         nc.sync.dma_start(
             out=ws_raw[:, 1, :].bitcast(I32), in_=wa_scales[0].bitcast(I32).unsqueeze(1).broadcast_to([16, 2, R // 4])
         )
-        nc.sync.dma_start(out=win2w[:], in_=tab2_words[0].rearrange("p t i -> p (t i)").bitcast(I32))
+        nc.sync.dma_start(list1[:], offs)
         en_v = en.rearrange("(u t e) n -> e u t n", t=4, e=2)
         for e in range(2):
             nc.sync.dma_start(out=en_raw[e:P:2, :, :], in_=en_v[e])
-        nc.sync.dma_start(out=wb_raw[:], in_=wb_words.rearrange("a p c -> p a c").bitcast(I32))
         nc.sync.dma_start(out=win1w[:], in_=tab_words[0].rearrange("p t i -> p (t i)").bitcast(I32))
         nc.sync.dma_start(out=wa_raw[:], in_=wa_words[0].bitcast(I32))
-        nc.gpsimd.dma_start(out=bias[:], in_=b.rearrange("(p m) -> p m", m=4))
+        for q in range(4):
+            nc.gpsimd.dma_start(
+                out=win1s[32 * q : 32 * q + 4, :].bitcast(I32), in_=tab_scales[0, 4 * q : 4 * q + 4, :].bitcast(I32)
+            )
 
         nc.scalar.activation(out=zero[:], in_=zin[:], func=ACT.Gelu_apprx_tanh)
 
         nc.vector.tensor_copy(g2s[:], win2s[:].indirect(list2[:]))
-        nc.vector.tensor_copy(g1s[:], win1s[:].indirect(list1[:]))
         nc.vector.tensor_copy(
-            out=stage[:, 1:4:2, :].bitcast(U16).rearrange("p a (t c i) -> p a c t i", t=4, i=4),
+            out=stage[:, 1:3, :].bitcast(U16).rearrange("p a (t c i) -> p a c t i", t=4, i=4),
             in_=ws_raw[:].bitcast(U16).rearrange("p a (c i t) -> p a c t i", t=4, i=4),
         )
         nc.vector.tensor_copy(out=stage[:, 0, :].bitcast(I32), in_=g2s[0:32, :].bitcast(I32))
-        nc.vector.tensor_copy(out=stage[:, 2, :].bitcast(I32), in_=g1s[0:32, :].bitcast(I32))
         for q in range(4):
             nc.scalar.dma_start(
                 out=planes[32 * q : 32 * q + 4, :, :].rearrange("p (a s) r -> p a (s r)", a=2).bitcast(I32),
                 in_=stage[8 * q : 8 * q + 8, :, :].rearrange("p s r -> p (s r)").bitcast(I32),
             )
+        bias = keep.tile([P, 4], F32, name="bias", tag="ws_then_bias", align_bytes=64)
+        nc.scalar.dma_start(out=bias[:], in_=b.rearrange("(p m) -> p m", m=4))
 
         cols = CH // 16
-        g2w, p2w, g1w = [], [], []
-        for c in range(NCH):
-            g = keep.tile([P, CH], U32, name="g2w%d" % c, align_bytes=64)
-            nc.vector.tensor_copy(g[:], win2w[:].bitcast(U32).indirect(list2[:, c * cols : (c + 1) * cols]))
-            g2w.append(g)
-        nc.vector.tensor_copy(
-            out=wb_p[:].rearrange("p a t (c i) -> p a c t i", i=4),
-            in_=wb_raw[:].rearrange("p a (c i t) -> p a c t i", t=4, i=4),
-        )
-        for c in range(NCH):
-            pw = keep.tile([P, 2, CH], U16, name="p2w%d" % c, align_bytes=64)
-            nc.vector.tensor_copy(out=pw[:], in_=g2w[c][:].bitcast(U16).rearrange("p (j d) -> p d j", d=2))
-            p2w.append(pw)
+        out_v = out.rearrange("(p m) j -> p m j", m=4)
+        th, ha, hbf = [], [], []
 
-        for k in range(4):
-            nc.scalar.copy(
-                out=en_bf[:].rearrange("p (m c) t -> p c t m", m=4)[:, 32 * k : 32 * k + 32, :, :],
-                in_=en_raw[:].rearrange("p t (c m) -> p c t m", m=4)[:, 32 * k : 32 * k + 32, :, :],
-            )
-
-        th = []
-        for c in range(NCH):
+        def project(c):
             js = slice(c * CH, (c + 1) * CH)
+            g2w = keep.tile([P, CH], U32, name="g2w%d" % c, align_bytes=64)
+            nc.vector.tensor_copy(g2w[:], win2w[:].bitcast(U32).indirect(list2[:, c * cols : (c + 1) * cols]))
+            if c == 0:
+                nc.vector.tensor_copy(
+                    out=wb_p[:].rearrange("p a t (c i) -> p a c t i", i=4),
+                    in_=wb_raw[:].rearrange("p a (c i t) -> p a c t i", t=4, i=4),
+                )
+            p2w = keep.tile([P, 2, CH], U16, name="p2w%d" % c, align_bytes=64)
+            nc.vector.tensor_copy(out=p2w[:], in_=g2w[:].bitcast(U16).rearrange("p (j d) -> p d j", d=2))
+            if c == 0:
+                nc.vector.tensor_copy(g1s[:], win1s[:].indirect(list1[:]))
+                nc.vector.tensor_copy(
+                    out=wa_p[:].rearrange("p t (c i) -> p c t i", i=4),
+                    in_=wa_raw[:].rearrange("p (c i t) -> p c t i", t=4, i=4),
+                )
+            g1w = keep.tile([P, CH], U32, name="g1w%d" % c, align_bytes=64)
+            nc.vector.tensor_copy(g1w[:], win1w[:].bitcast(U32).indirect(list1[:, c * cols : (c + 1) * cols]))
             hb = psum.tile([P, 4, CH], F32, name="hb", tag="hb", bufs=3)
             for t in range(4):
                 for a in range(2):
                     nc.tensor.matmul_mx(
                         out=hb[:, t, :],
                         lhsT=wb_p[:, a, t, :].bitcast(FP4X4),
-                        lhsT_scale=planes[:, 4 * a + 1, t * P : (t + 1) * P],
-                        rhs=p2w[c][:, a, :].bitcast(FP4X4),
-                        rhs_scale=planes[:, 4 * a, js],
+                        lhsT_scale=planes[:, 3 * a + 1, t * P : (t + 1) * P],
+                        rhs=p2w[:, a, :].bitcast(FP4X4),
+                        rhs_scale=planes[:, 3 * a, js],
                         start=(a == 0),
                         stop=(a == 1),
                     )
@@ -133,35 +130,18 @@ def tile_list_kg_gate_gelu_kernel(
                 out=tt[:], in_=hb[:].rearrange("p t j -> p j t"), func=ACT.Tanh, scale=0.5, bias=zero[:]
             )
             th.append(tt)
-
-        nc.vector.tensor_copy(
-            out=wa_p[:].rearrange("p t (c i) -> p c t i", i=4),
-            in_=wa_raw[:].rearrange("p (c i t) -> p c t i", t=4, i=4),
-        )
-        for c in range(NCH):
-            g = keep.tile([P, CH], U32, name="g1w%d" % c, align_bytes=64)
-            nc.vector.tensor_copy(g[:], win1w[:].bitcast(U32).indirect(list1[:, c * cols : (c + 1) * cols]))
-            g1w.append(g)
-        nc.vector.quantize_mx(out=en_q[:].bitcast(FP8X4), scales=en_s[:], in_=en_bf[:].rearrange("p n t -> p (n t)"))
-
-        ha = []
-        for c in range(NCH):
-            js = slice(c * CH, (c + 1) * CH)
             acc = psum.tile([P, 4, CH], F32, name="ha", tag="ha", bufs=3)
             for t in range(4):
                 nc.tensor.matmul_mx(
                     out=acc[:, t, :],
                     lhsT=wa_p[:, t, :].bitcast(FP4X4),
-                    lhsT_scale=planes[:, 3, t * P : (t + 1) * P],
-                    rhs=g1w[c][:].bitcast(FP8X4),
-                    rhs_scale=planes[:, 2, js],
+                    lhsT_scale=planes[:, 2, t * P : (t + 1) * P],
+                    rhs=g1w[:].bitcast(FP8X4),
+                    rhs_scale=g1s[:, js],
                     start=True,
                     stop=True,
                 )
             ha.append(acc)
-
-        out_v = out.rearrange("(p m) j -> p m j", m=4)
-        hbf = []
 
         def gate(c):
             h = keep.tile([P, CH, 4], BF16, name="h%d" % c, align_bytes=64)
@@ -186,14 +166,30 @@ def tile_list_kg_gate_gelu_kernel(
                     start=True,
                     stop=True,
                 )
-            for m in range(4):
-                nc.scalar.activation(
-                    out=res[:, m, :], in_=y[:, m, :], func=ACT.Gelu_apprx_tanh, scale=0.5, bias=bias[:, m : m + 1]
+            parts = 2 if c == NCH - 1 else 1
+            for part in range(parts):
+                ms = range(part * 4 // parts, (part + 1) * 4 // parts)
+                for m in ms:
+                    nc.scalar.activation(
+                        out=res[:, m, :], in_=y[:, m, :], func=ACT.Gelu_apprx_tanh, scale=0.5, bias=bias[:, m : m + 1]
+                    )
+                nc.sync.dma_start(
+                    out=out_v[:, ms.start : ms.stop, c * CH : (c + 1) * CH], in_=res[:, ms.start : ms.stop, :]
                 )
-            nc.sync.dma_start(out=out_v[:, :, c * CH : (c + 1) * CH], in_=res[:])
 
-        gate(0)
-        for c in range(1, NCH):
-            gate(c)
-            score(c - 1)
-        score(NCH - 1)
+        for k in range(2):
+            nc.scalar.copy(
+                out=en_bf[:].rearrange("p (m c) t -> p c m t", m=4)[:, 64 * k : 64 * k + 64, :, :],
+                in_=en_raw[:].rearrange("p t (c m) -> p c m t", m=4)[:, 64 * k : 64 * k + 64, :, :],
+            )
+        for step in range(NCH + 2):
+            if step < NCH:
+                project(step)
+            if 1 <= step <= NCH:
+                gate(step - 1)
+            if step == 1:
+                nc.vector.quantize_mx(
+                    out=en_q[:].bitcast(FP8X4), scales=en_s[:], in_=en_bf[:].rearrange("p n t -> p (n t)")
+                )
+            if step >= 2:
+                score(step - 2)

@@ -33,95 +33,121 @@ def tile_list_kg_gate_gelu_kernel(
         win2s = keep.tile([P, T], U8, name="win2s", align_bytes=64)
         win1s = keep.tile([P, T], U8, name="win1s", align_bytes=64)
         win2w = keep.tile([P, T], I32, name="win2w", align_bytes=64)
-        win1w = keep.tile([P, T], I32, name="win1w", align_bytes=64)
-        ws_raw = keep.tile([32, 2, R], U8, name="ws_raw", tag="ws_then_bias", align_bytes=64)
+        ws_raw = keep.tile([32, 2, R], U8, name="ws_raw", align_bytes=64)
         wb_raw = keep.tile([P, 2, R // 2], I32, name="wb_raw", align_bytes=64)
         wa_raw = keep.tile([P, R // 2], I32, name="wa_raw", align_bytes=64)
         en_raw = keep.tile([P, 4, N], F32, name="en_raw", align_bytes=64)
         zin = keep.tile([P, 1], F32, name="zin")
         zero = keep.tile([P, 1], F32, name="zero")
-        planes = keep.tile([P, 6, 512], U8, name="planes", align_bytes=64)
-        stage = keep.tile([32, 3, 512], U8, name="stage", align_bytes=64)
-        g2s = keep.tile([P, J], U8, name="g2s", align_bytes=64)
-        g1s = keep.tile([P, J], U8, name="g1s", align_bytes=64)
         wb_p = keep.tile([P, 2, 4, 64], I32, name="wb_p", align_bytes=64)
         wa_p = keep.tile([P, 4, 64], I32, name="wa_p", align_bytes=64)
         en_bf = keep.tile([P, N, 4], BF16, name="en_bf", align_bytes=64)
-        en_q = keep.tile([P, N], U32, name="en_q", align_bytes=64)
         en_s = keep.tile([P, N], U8, name="en_s", align_bytes=64)
 
-        nc.vector.memset(win2s[32:64, :].bitcast(I32), 0)
-        nc.vector.memset(win2s[64:128, :].bitcast(I32), 0)
-        nc.gpsimd.memset(win1s[:].bitcast(I32), 0)
+        for win in (win2s, win1s):
+            nc.vector.memset(win[32:64, :].bitcast(I32), 0)
+            nc.vector.memset(win[64:128, :].bitcast(I32), 0)
         nc.vector.memset(zin[:], 0.0)
 
         nc.sync.dma_start(list2[:], offs2)
-        nc.scalar.dma_start(out=win2w[:], in_=tab2_words[0].rearrange("p t i -> p (t i)").bitcast(I32))
+        nc.scalar.dma_start(out=ws_raw[:, 0, :].bitcast(I32), in_=wb_scales.rearrange("a q r -> q a r").bitcast(I32))
         nc.sync.dma_start(out=win2s[0:32, :].bitcast(I32), in_=tab2_scales.rearrange("a q t -> q a t").bitcast(I32))
-        nc.scalar.dma_start(out=wb_raw[:], in_=wb_words.rearrange("a p c -> p a c").bitcast(I32))
-        nc.sync.dma_start(out=ws_raw[:, 0, :].bitcast(I32), in_=wb_scales.rearrange("a q r -> q a r").bitcast(I32))
-        nc.sync.dma_start(
+        nc.scalar.dma_start(
             out=ws_raw[:, 1, :].bitcast(I32), in_=wa_scales[0].bitcast(I32).unsqueeze(1).broadcast_to([16, 2, R // 4])
         )
         nc.sync.dma_start(list1[:], offs)
+        nc.scalar.dma_start(
+            out=win1s[0:32, :].bitcast(I32), in_=tab_scales[0].bitcast(I32).unsqueeze(1).broadcast_to([16, 2, T // 4])
+        )
         en_v = en.rearrange("(u t e) n -> e u t n", t=4, e=2)
-        for e in range(2):
-            nc.sync.dma_start(out=en_raw[e:P:2, :, :], in_=en_v[e])
-        nc.sync.dma_start(out=win1w[:], in_=tab_words[0].rearrange("p t i -> p (t i)").bitcast(I32))
-        nc.sync.dma_start(out=wa_raw[:], in_=wa_words[0].bitcast(I32))
-        for q in range(4):
-            nc.gpsimd.dma_start(
-                out=win1s[32 * q : 32 * q + 4, :].bitcast(I32), in_=tab_scales[0, 4 * q : 4 * q + 4, :].bitcast(I32)
-            )
+        nc.sync.dma_start(out=en_raw[0:P:2, :, :], in_=en_v[0])
+        nc.sync.dma_start(out=wb_raw[:], in_=wb_words.rearrange("a p c -> p a c").bitcast(I32))
+        nc.sync.dma_start(out=win2w[:], in_=tab2_words[0].rearrange("p t i -> p (t i)").bitcast(I32))
+        nc.sync.dma_start(out=en_raw[1:P:2, :, :], in_=en_v[1])
 
         nc.scalar.activation(out=zero[:], in_=zin[:], func=ACT.Gelu_apprx_tanh)
 
-        nc.vector.tensor_copy(g2s[:], win2s[:].indirect(list2[:]))
-        nc.vector.tensor_copy(
-            out=stage[:, 1:3, :].bitcast(U16).rearrange("p a (t c i) -> p a c t i", t=4, i=4),
-            in_=ws_raw[:].bitcast(U16).rearrange("p a (c i t) -> p a c t i", t=4, i=4),
-        )
-        nc.vector.tensor_copy(out=stage[:, 0, :].bitcast(I32), in_=g2s[0:32, :].bitcast(I32))
-        for q in range(4):
-            nc.scalar.dma_start(
-                out=planes[32 * q : 32 * q + 4, :, :].rearrange("p (a s) r -> p a (s r)", a=2).bitcast(I32),
-                in_=stage[8 * q : 8 * q + 8, :, :].rearrange("p s r -> p (s r)").bitcast(I32),
-            )
-        bias = keep.tile([P, 4], F32, name="bias", tag="ws_then_bias", align_bytes=64)
-        nc.scalar.dma_start(out=bias[:], in_=b.rearrange("(p m) -> p m", m=4))
+        HALF = J // 2
+        planes = []
+        for half in range(2):
+            lo = 2 * R if half == 0 else 0
+            width = lo + 2 * HALF
+            plane = keep.tile([P, 2, width], U8, name="planes%d" % half, align_bytes=64)
+            gs = keep.tile([P, 2, HALF], U8, name="gs%d" % half, tag="gs", align_bytes=64)
+            entries = slice(half * HALF // 16, (half + 1) * HALF // 16)
+            if half == 0:
+                stage = keep.tile([32, width], U8, name="stage", align_bytes=64)
+                nc.vector.tensor_copy(
+                    out=stage[:, 0:lo].bitcast(U16).rearrange("p (a t c i) -> p a c t i", a=2, t=4, i=4),
+                    in_=ws_raw[:].bitcast(U16).rearrange("p a (c i t) -> p a c t i", t=4, i=4),
+                )
+            nc.vector.tensor_copy(gs[:, 0, :], win2s[:].indirect(list2[:, entries]))
+            nc.vector.tensor_copy(gs[:, 1, :], win1s[:].indirect(list1[:, entries]))
+            rows = gs[0:32, :, :].rearrange("p s j -> p (s j)").bitcast(I32)
+            if half == 0:
+                nc.vector.tensor_copy(out=stage[:, lo:].bitcast(I32), in_=rows)
+                rows = stage[:].bitcast(I32)
+            if half == 1:
+                nc.sync.dma_start(out=wa_raw[:], in_=wa_words[0].bitcast(I32))
+                win1w = keep.tile([P, T], I32, name="win1w", align_bytes=64)
+                nc.sync.dma_start(out=win1w[:], in_=tab_words[0].rearrange("p t i -> p (t i)").bitcast(I32))
+            for q in range(4):
+                nc.sync.dma_start(
+                    out=plane[32 * q : 32 * q + 4, :, :].bitcast(I32), in_=rows[8 * q : 8 * q + 8, :]
+                )
+            planes.append(plane)
+
+        bias = keep.tile([P, 4], F32, name="bias")
+        nc.sync.dma_start(out=bias[:], in_=b.rearrange("(p m) -> p m", m=4))
 
         cols = CH // 16
         out_v = out.rearrange("(p m) j -> p m j", m=4)
-        th, ha, hbf = [], [], []
+        th, ha, hbf, words1, words2 = [], [], [], [], []
+        nc.gpsimd.tensor_copy(
+            out=wb_p[:].rearrange("p a t (c i) -> p a c t i", i=4),
+            in_=wb_raw[:].rearrange("p a (c i t) -> p a c t i", t=4, i=4),
+        )
+        nc.gpsimd.tensor_copy(
+            out=wa_p[:].rearrange("p t (c i) -> p c t i", i=4),
+            in_=wa_raw[:].rearrange("p (c i t) -> p c t i", t=4, i=4),
+        )
 
         def project(c):
-            js = slice(c * CH, (c + 1) * CH)
-            g2w = keep.tile([P, CH], U32, name="g2w%d" % c, align_bytes=64)
-            nc.vector.tensor_copy(g2w[:], win2w[:].bitcast(U32).indirect(list2[:, c * cols : (c + 1) * cols]))
-            if c == 0:
+            plane = planes[c // 2]
+            at = (2 * R if c < 2 else 0) + (c % 2) * CH
+            if c % 2 == 0:
+                entries = slice(c * cols, (c + 2) * cols)
+                g2w = keep.tile([P, 2 * CH], U32, name="g2w%d" % c, tag="g2w", align_bytes=64)
+                nc.vector.tensor_copy(g2w[:], win2w[:].bitcast(U32).indirect(list2[:, entries]))
+                pairs = g2w[:].bitcast(U16).rearrange("p (c j d) -> p c d j", c=2, d=2)
+                if c == 0:
+                    for k in range(2):
+                        parted = keep.tile([P, 2, CH], U16, name="p2w%d" % k, align_bytes=64)
+                        nc.vector.tensor_copy(out=parted[:], in_=pairs[:, k, :, :])
+                        words2.append(parted[:])
+                else:
+                    parted = keep.tile([P, 2, 2, CH], U16, name="p2w23", tag="g1w0", align_bytes=64)
+                    nc.vector.tensor_copy(out=parted[:], in_=pairs)
+                    words2.extend([parted[:, 0, :, :], parted[:, 1, :, :]])
+            if c < 2:
+                count = 1 if c == 0 else NCH - 1
+                picked = keep.tile([P, count, CH], U32, name="g1w%d" % c, tag="g1w%d" % c, align_bytes=64)
                 nc.vector.tensor_copy(
-                    out=wb_p[:].rearrange("p a t (c i) -> p a c t i", i=4),
-                    in_=wb_raw[:].rearrange("p a (c i t) -> p a c t i", t=4, i=4),
+                    picked[:].rearrange("p c j -> p (c j)"),
+                    win1w[:].bitcast(U32).indirect(list1[:, c * cols : (c + count) * cols]),
                 )
-            p2w = keep.tile([P, 2, CH], U16, name="p2w%d" % c, align_bytes=64)
-            nc.vector.tensor_copy(out=p2w[:], in_=g2w[:].bitcast(U16).rearrange("p (j d) -> p d j", d=2))
-            if c == 0:
-                nc.vector.tensor_copy(g1s[:], win1s[:].indirect(list1[:]))
-                nc.vector.tensor_copy(
-                    out=wa_p[:].rearrange("p t (c i) -> p c t i", i=4),
-                    in_=wa_raw[:].rearrange("p (c i t) -> p c t i", t=4, i=4),
-                )
-            g1w = keep.tile([P, CH], U32, name="g1w%d" % c, align_bytes=64)
-            nc.vector.tensor_copy(g1w[:], win1w[:].bitcast(U32).indirect(list1[:, c * cols : (c + 1) * cols]))
-            hb = psum.tile([P, 4, CH], F32, name="hb", tag="hb", bufs=3)
+                words1.extend([picked[:, k, :] for k in range(count)])
+            p2w = words2[c]
+            g1w = words1[c]
+            hb = psum.tile([P, 4, CH], F32, name="hb%d" % c, tag="bank%d" % c)
             for t in range(4):
                 for a in range(2):
                     nc.tensor.matmul_mx(
                         out=hb[:, t, :],
                         lhsT=wb_p[:, a, t, :].bitcast(FP4X4),
-                        lhsT_scale=planes[:, 3 * a + 1, t * P : (t + 1) * P],
+                        lhsT_scale=planes[0][:, a, t * P : (t + 1) * P],
                         rhs=p2w[:, a, :].bitcast(FP4X4),
-                        rhs_scale=planes[:, 3 * a, js],
+                        rhs_scale=plane[:, a, at : at + CH],
                         start=(a == 0),
                         stop=(a == 1),
                     )
@@ -130,14 +156,14 @@ def tile_list_kg_gate_gelu_kernel(
                 out=tt[:], in_=hb[:].rearrange("p t j -> p j t"), func=ACT.Tanh, scale=0.5, bias=zero[:]
             )
             th.append(tt)
-            acc = psum.tile([P, 4, CH], F32, name="ha", tag="ha", bufs=3)
+            acc = psum.tile([P, 4, CH], F32, name="ha%d" % c, tag="bank%d" % ((c + 4) % 6))
             for t in range(4):
                 nc.tensor.matmul_mx(
                     out=acc[:, t, :],
                     lhsT=wa_p[:, t, :].bitcast(FP4X4),
-                    lhsT_scale=planes[:, 2, t * P : (t + 1) * P],
-                    rhs=g1w[:].bitcast(FP8X4),
-                    rhs_scale=g1s[:, js],
+                    lhsT_scale=planes[0][:, 0, R + t * P : R + (t + 1) * P],
+                    rhs=g1w.bitcast(FP8X4),
+                    rhs_scale=plane[:, 0, at + HALF : at + HALF + CH],
                     start=True,
                     stop=True,
                 )
@@ -154,7 +180,7 @@ def tile_list_kg_gate_gelu_kernel(
             hq = keep.tile([P, CH], U32, name="hq%d" % c, align_bytes=64)
             hs = keep.tile([P, CH], U8, name="hs%d" % c, align_bytes=64)
             nc.vector.quantize_mx(out=hq[:].bitcast(FP8X4), scales=hs[:], in_=hbf[c][:].rearrange("p j t -> p (j t)"))
-            y = psum.tile([P, 4, CH], F32, name="y", tag="y", bufs=2)
+            y = psum.tile([P, 4, CH], F32, name="y%d" % c, tag="bank%d" % ((c + 6) if c < 2 else c))
             res = keep.tile([P, 4, CH], F32, name="res%d" % c, align_bytes=64)
             for m in range(4):
                 nc.tensor.matmul_mx(
@@ -187,9 +213,12 @@ def tile_list_kg_gate_gelu_kernel(
                 project(step)
             if 1 <= step <= NCH:
                 gate(step - 1)
-            if step == 1:
+            if step == NCH - 1:
+                en_q = keep.tile([P, N], U32, name="en_q", tag="g2w", align_bytes=64)
                 nc.vector.quantize_mx(
                     out=en_q[:].bitcast(FP8X4), scales=en_s[:], in_=en_bf[:].rearrange("p n t -> p (n t)")
                 )
-            if step >= 2:
+            if step == NCH - 1:
+                score(0)
+            if step >= NCH - 1:
                 score(step - 2)

@@ -62,8 +62,11 @@ def tile_list_kg_gate_gelu_kernel(
         en_v = en.rearrange("(u t e) n -> e u t n", t=4, e=2)
         nc.sync.dma_start(out=en_raw[0:P:2, :, :], in_=en_v[0])
         nc.sync.dma_start(out=wb_raw[:], in_=wb_words.rearrange("a p c -> p a c").bitcast(I32))
+        nc.sync.dma_start(out=wa_raw[:], in_=wa_words[0].bitcast(I32))
         nc.sync.dma_start(out=win2w[:], in_=tab2_words[0].rearrange("p t i -> p (t i)").bitcast(I32))
         nc.sync.dma_start(out=en_raw[1:P:2, :, :], in_=en_v[1])
+        win1w = keep.tile([P, T], I32, name="win1w", tag="win1w", align_bytes=64)
+        nc.sync.dma_start(out=win1w[:], in_=tab_words[0].rearrange("p t i -> p (t i)").bitcast(I32))
 
         nc.scalar.activation(out=zero[:], in_=zin[:], func=ACT.Gelu_apprx_tanh)
 
@@ -87,10 +90,6 @@ def tile_list_kg_gate_gelu_kernel(
             if half == 0:
                 nc.vector.tensor_copy(out=stage[:, lo:].bitcast(I32), in_=rows)
                 rows = stage[:].bitcast(I32)
-            if half == 1:
-                nc.sync.dma_start(out=wa_raw[:], in_=wa_words[0].bitcast(I32))
-                win1w = keep.tile([P, T], I32, name="win1w", align_bytes=64)
-                nc.sync.dma_start(out=win1w[:], in_=tab_words[0].rearrange("p t i -> p (t i)").bitcast(I32))
             for q in range(4):
                 nc.sync.dma_start(
                     out=plane[32 * q : 32 * q + 4, :, :].bitcast(I32), in_=rows[8 * q : 8 * q + 8, :]
@@ -120,18 +119,13 @@ def tile_list_kg_gate_gelu_kernel(
                 g2w = keep.tile([P, 2 * CH], U32, name="g2w%d" % c, tag="g2w", align_bytes=64)
                 nc.vector.tensor_copy(g2w[:], win2w[:].bitcast(U32).indirect(list2[:, entries]))
                 pairs = g2w[:].bitcast(U16).rearrange("p (c j d) -> p c d j", c=2, d=2)
-                if c == 0:
-                    for k in range(2):
-                        parted = keep.tile([P, 2, CH], U16, name="p2w%d" % k, align_bytes=64)
-                        nc.vector.tensor_copy(out=parted[:], in_=pairs[:, k, :, :])
-                        words2.append(parted[:])
-                else:
-                    parted = keep.tile([P, 2, 2, CH], U16, name="p2w23", tag="g1w0", align_bytes=64)
-                    nc.vector.tensor_copy(out=parted[:], in_=pairs)
-                    words2.extend([parted[:, 0, :, :], parted[:, 1, :, :]])
+                for k in range(2):
+                    parted = keep.tile([P, 2, CH], U16, name="p2w%d" % (c + k), align_bytes=64)
+                    nc.vector.tensor_copy(out=parted[:], in_=pairs[:, k, :, :])
+                    words2.append(parted[:])
             if c < 2:
                 count = 1 if c == 0 else NCH - 1
-                picked = keep.tile([P, count, CH], U32, name="g1w%d" % c, tag="g1w%d" % c, align_bytes=64)
+                picked = keep.tile([P, count, CH], U32, name="g1w%d" % c, align_bytes=64)
                 nc.vector.tensor_copy(
                     picked[:].rearrange("p c j -> p (c j)"),
                     win1w[:].bitcast(U32).indirect(list1[:, c * cols : (c + count) * cols]),
@@ -213,12 +207,10 @@ def tile_list_kg_gate_gelu_kernel(
                 project(step)
             if 1 <= step <= NCH:
                 gate(step - 1)
-            if step == NCH - 1:
-                en_q = keep.tile([P, N], U32, name="en_q", tag="g2w", align_bytes=64)
+            if step == 1:
+                en_q = keep.tile([P, N], U32, name="en_q", tag="win1w", align_bytes=64)
                 nc.vector.quantize_mx(
                     out=en_q[:].bitcast(FP8X4), scales=en_s[:], in_=en_bf[:].rearrange("p n t -> p (n t)")
                 )
-            if step == NCH - 1:
-                score(0)
-            if step >= NCH - 1:
+            if step >= 2:
                 score(step - 2)

from contextlib import ExitStack

import concourse.mybir as mybir

F32 = mybir.dt.float32
BF16 = mybir.dt.bfloat16
I32 = mybir.dt.int32
U32 = mybir.dt.uint32
U16 = mybir.dt.uint16
U8 = mybir.dt.uint8
FP8X4 = mybir.dt.float8_e4m3fn_x4
FP4X4 = mybir.dt.float4_e2m1fn_x4
ACT = mybir.ActivationFunctionType
ALU = mybir.AluOpType

K, L, R, N, T, J = 512, 1024, 512, 512, 1024, 512
P = 128
CH = 128
NCH = J // CH
FLOPS = 2 * J * (K * R + L * R + R * N)


def tile_list_kg_gate_gelu_kernel(
    tc, tab_words, tab_scales, tab2_words, tab2_scales, wa_words, wa_scales, wb_words, wb_scales, en, b, offs, offs2, out
):
    nc = tc.nc
    with ExitStack() as ctx:
        keep = ctx.enter_context(tc.tile_pool(name="keep", bufs=1))
        psum = ctx.enter_context(tc.psum_pool(name="psum", bufs=1))

        list1 = keep.tile([P, J // 16], U16, name="list1")
        list2 = keep.tile([P, J // 16], U16, name="list2")
        win2s = keep.tile([P, T], U8, name="win2s", align_bytes=64)
        win1s = keep.tile([P, T], U8, name="win1s", align_bytes=64)
        win2w = keep.tile([P, T], I32, name="win2w", align_bytes=64)
        ws_raw = keep.tile([32, 2, R], U8, name="ws_raw", align_bytes=64)
        wb_raw = keep.tile([P, 2, R // 2], I32, name="wb_raw", align_bytes=64)
        wa_raw = keep.tile([P, R // 2], I32, name="wa_raw", align_bytes=64)
        en_raw = keep.tile([P, 4, N], F32, name="en_raw", align_bytes=64)
        zin = keep.tile([P, 1], F32, name="zin")
        zero = keep.tile([P, 1], F32, name="zero")
        wb_p = keep.tile([P, 2, 4, 64], I32, name="wb_p", align_bytes=64)
        wa_p = keep.tile([P, 4, 64], I32, name="wa_p", align_bytes=64)
        en_bf = keep.tile([P, N, 4], BF16, name="en_bf", align_bytes=64)
        en_s = keep.tile([P, N], U8, name="en_s", align_bytes=64)

        for win in (win2s, win1s):
            nc.vector.memset(win[32:64, :].bitcast(I32), 0)
            nc.vector.memset(win[64:128, :].bitcast(I32), 0)
        nc.vector.memset(zin[:], 0.0)

        nc.sync.dma_start(list2[:], offs2)
        nc.scalar.dma_start(out=ws_raw[:, 0, :].bitcast(I32), in_=wb_scales.rearrange("a q r -> q a r").bitcast(I32))
        nc.sync.dma_start(out=win2s[0:32, :].bitcast(I32), in_=tab2_scales.rearrange("a q t -> q a t").bitcast(I32))
        nc.scalar.dma_start(
            out=ws_raw[:, 1, :].bitcast(I32), in_=wa_scales[0].bitcast(I32).unsqueeze(1).broadcast_to([16, 2, R // 4])
        )
        nc.sync.dma_start(list1[:], offs)
        nc.scalar.dma_start(
            out=win1s[0:32, :].bitcast(I32), in_=tab_scales[0].bitcast(I32).unsqueeze(1).broadcast_to([16, 2, T // 4])
        )
        en_v = en.rearrange("(u t e) n -> e u t n", t=4, e=2)
        nc.sync.dma_start(out=en_raw[0:P:2, :, :], in_=en_v[0])
        nc.sync.dma_start(out=wb_raw[:], in_=wb_words.rearrange("a p c -> p a c").bitcast(I32))
        nc.sync.dma_start(out=wa_raw[:], in_=wa_words[0].bitcast(I32))
        nc.sync.dma_start(out=win2w[:], in_=tab2_words[0].rearrange("p t i -> p (t i)").bitcast(I32))
        nc.sync.dma_start(out=en_raw[1:P:2, :, :], in_=en_v[1])
        win1w = keep.tile([P, T], I32, name="win1w", tag="win1w", align_bytes=64)
        nc.sync.dma_start(out=win1w[:], in_=tab_words[0].rearrange("p t i -> p (t i)").bitcast(I32))

        nc.scalar.activation(out=zero[:], in_=zin[:], func=ACT.Gelu_apprx_tanh)

        HALF = J // 2
        planes = []
        for half in range(2):
            lo = 2 * R if half == 0 else 0
            width = lo + 2 * HALF
            plane = keep.tile([P, 2, width], U8, name="planes%d" % half, align_bytes=64)
            gs = keep.tile([P, 2, HALF], U8, name="gs%d" % half, tag="gs", align_bytes=64)
            entries = slice(half * HALF // 16, (half + 1) * HALF // 16)
            if half == 0:
                stage = keep.tile([32, width], U8, name="stage", align_bytes=64)
                nc.vector.tensor_copy(
                    out=stage[:, 0:lo].bitcast(U16).rearrange("p (a t c i) -> p a c t i", a=2, t=4, i=4),
                    in_=ws_raw[:].bitcast(U16).rearrange("p a (c i t) -> p a c t i", t=4, i=4),
                )
            nc.vector.tensor_copy(gs[:, 0, :], win2s[:].indirect(list2[:, entries]))
            nc.vector.tensor_copy(gs[:, 1, :], win1s[:].indirect(list1[:, entries]))
            rows = gs[0:32, :, :].rearrange("p s j -> p (s j)").bitcast(I32)
            if half == 0:
                nc.vector.tensor_copy(out=stage[:, lo:].bitcast(I32), in_=rows)
                rows = stage[:].bitcast(I32)
            for q in range(4):
                nc.sync.dma_start(
                    out=plane[32 * q : 32 * q + 4, :, :].bitcast(I32), in_=rows[8 * q : 8 * q + 8, :]
                )
            planes.append(plane)

        bias = keep.tile([P, 4], F32, name="bias")
        nc.sync.dma_start(out=bias[:], in_=b.rearrange("(p m) -> p m", m=4))

        cols = CH // 16
        out_v = out.rearrange("(p m) j -> p m j", m=4)
        th, ha, hbf, words1, words2 = [], [], [], [], []
        nc.gpsimd.tensor_copy(
            out=wb_p[:].rearrange("p a t (c i) -> p a c t i", i=4),
            in_=wb_raw[:].rearrange("p a (c i t) -> p a c t i", t=4, i=4),
        )
        nc.gpsimd.tensor_copy(
            out=wa_p[:].rearrange("p t (c i) -> p c t i", i=4),
            in_=wa_raw[:].rearrange("p (c i t) -> p c t i", t=4, i=4),
        )

        def project(c):
            plane = planes[c // 2]
            at = (2 * R if c < 2 else 0) + (c % 2) * CH
            if c % 2 == 0:
                entries = slice(c * cols, (c + 2) * cols)
                g2w = keep.tile([P, 2 * CH], U32, name="g2w%d" % c, tag="g2w", align_bytes=64)
                nc.vector.tensor_copy(g2w[:], win2w[:].bitcast(U32).indirect(list2[:, entries]))
                pairs = g2w[:].bitcast(U16).rearrange("p (c j d) -> p c d j", c=2, d=2)
                for k in range(2):
                    parted = keep.tile([P, 2, CH], U16, name="p2w%d" % (c + k), align_bytes=64)
                    nc.vector.tensor_copy(out=parted[:], in_=pairs[:, k, :, :])
                    words2.append(parted[:])
            if c < 2:
                count = 1 if c == 0 else NCH - 1
                picked = keep.tile([P, count, CH], U32, name="g1w%d" % c, align_bytes=64)
                nc.vector.tensor_copy(
                    picked[:].rearrange("p c j -> p (c j)"),
                    win1w[:].bitcast(U32).indirect(list1[:, c * cols : (c + count) * cols]),
                )
                words1.extend([picked[:, k, :] for k in range(count)])
            p2w = words2[c]
            g1w = words1[c]
            hb = psum.tile([P, 4, CH], F32, name="hb%d" % c, tag="bank%d" % c)
            for t in range(4):
                for a in range(2):
                    nc.tensor.matmul_mx(
                        out=hb[:, t, :],
                        lhsT=wb_p[:, a, t, :].bitcast(FP4X4),
                        lhsT_scale=planes[0][:, a, t * P : (t + 1) * P],
                        rhs=p2w[:, a, :].bitcast(FP4X4),
                        rhs_scale=plane[:, a, at : at + CH],
                        start=(a == 0),
                        stop=(a == 1),
                    )
            tt = keep.tile([P, CH, 4], F32, name="th%d" % c, align_bytes=64)
            nc.scalar.activation(
                out=tt[:], in_=hb[:].rearrange("p t j -> p j t"), func=ACT.Tanh, scale=0.5, bias=zero[:]
            )
            th.append(tt)
            acc = psum.tile([P, 4, CH], F32, name="ha%d" % c, tag="bank%d" % ((c + 4) % 6))
            for t in range(4):
                nc.tensor.matmul_mx(
                    out=acc[:, t, :],
                    lhsT=wa_p[:, t, :].bitcast(FP4X4),
                    lhsT_scale=planes[0][:, 0, R + t * P : R + (t + 1) * P],
                    rhs=g1w.bitcast(FP8X4),
                    rhs_scale=plane[:, 0, at + HALF : at + HALF + CH],
                    start=True,
                    stop=True,
                )
            ha.append(acc)

        def gate(c):
            h = keep.tile([P, CH, 4], BF16, name="h%d" % c, align_bytes=64)
            nc.vector.scalar_tensor_tensor(
                out=h[:], in0=th[c][:], scalar=1.0, in1=ha[c][:].rearrange("p t j -> p j t"), op0=ALU.add, op1=ALU.mult
            )
            hbf.append(h)

        def score(c):
            hq = keep.tile([P, CH], U32, name="hq%d" % c, align_bytes=64)
            hs = keep.tile([P, CH], U8, name="hs%d" % c, align_bytes=64)
            nc.vector.quantize_mx(out=hq[:].bitcast(FP8X4), scales=hs[:], in_=hbf[c][:].rearrange("p j t -> p (j t)"))
            y = psum.tile([P, 4, CH], F32, name="y%d" % c, tag="bank%d" % ((c + 6) if c < 2 else c))
            res = keep.tile([P, 4, CH], F32, name="res%d" % c, align_bytes=64)
            for m in range(4):
                nc.tensor.matmul_mx(
                    out=y[:, m, :],
                    lhsT=en_q[:, m * P : (m + 1) * P].bitcast(FP8X4),
                    lhsT_scale=en_s[:, m * P : (m + 1) * P],
                    rhs=hq[:].bitcast(FP8X4),
                    rhs_scale=hs[:],
                    start=True,
                    stop=True,
                )
            parts = 2 if c == NCH - 1 else 1
            for part in range(parts):
                ms = range(part * 4 // parts, (part + 1) * 4 // parts)
                for m in ms:
                    nc.scalar.activation(
                        out=res[:, m, :], in_=y[:, m, :], func=ACT.Gelu_apprx_tanh, scale=0.5, bias=bias[:, m : m + 1]
                    )
                nc.sync.dma_start(
                    out=out_v[:, ms.start : ms.stop, c * CH : (c + 1) * CH], in_=res[:, ms.start : ms.stop, :]
                )

        for k in range(2):
            nc.scalar.copy(
                out=en_bf[:].rearrange("p (m c) t -> p c m t", m=4)[:, 64 * k : 64 * k + 64, :, :],
                in_=en_raw[:].rearrange("p t (c m) -> p c m t", m=4)[:, 64 * k : 64 * k + 64, :, :],
            )
        for step in range(NCH + 2):
            if step < NCH:
                project(step)
            if 1 <= step <= NCH:
                gate(step - 1)
            if step == 1:
                en_q = keep.tile([P, N], U32, name="en_q", tag="win1w", align_bytes=64)
                nc.vector.quantize_mx(
                    out=en_q[:].bitcast(FP8X4), scales=en_s[:], in_=en_bf[:].rearrange("p n t -> p (n t)")
                )
            if step >= 2:
                score(step - 2)
